import numpy as np
import ml_dtypes


def mxq(x, axis, fmt="e4m3"):
    dtype, down = {"e4m3": (ml_dtypes.float8_e4m3fn, 7), "e5m2": (ml_dtypes.float8_e5m2, 14)}[fmt]
    v = np.moveaxis(np.asarray(x, np.float32).astype(ml_dtypes.bfloat16).astype(np.float64), axis, -1)
    blocks = v.reshape(v.shape[:-1] + (-1, 32))
    amax = np.abs(blocks).max(-1, keepdims=True)
    byte = np.maximum(np.where(amax > 0, np.frexp(amax)[1] - 1 + 127, 0) - down, 1)
    scale = np.exp2(byte - 127.0)
    codes = (blocks / scale).astype(np.float32).astype(dtype).astype(np.float64)
    return np.moveaxis((codes * scale).reshape(v.shape), -1, axis)


WIDE = False


def mx_kscale(k):
    if not WIDE:
        return np.ones(k)
    levels = np.array([10, -10, 5, -5, 0])
    if k % 512:
        return np.exp2(np.random.permutation(np.resize(levels, k // 32))).repeat(32)
    a = np.empty((k // 512, 16))
    for p in range(k // 512):
        a[p, :8] = np.random.permutation(np.resize(levels, 8))
        for g in range(8):
            far = levels[np.abs(levels - a[p, g]) >= 10]
            a[p, g + 8] = far[np.random.randint(len(far))]
    return np.exp2(a.ravel()).repeat(32)


def f64(x):
    return np.asarray(x).astype(np.float64)


def striped(idx):
    return np.tile(np.asarray(idx).reshape(-1, 16).T, (8, 1)).astype(np.uint16)


def unstriped(offs):
    return offs[:16].T.reshape(-1).astype(np.int64)


E2M1 = np.array([0.0, 0.5, 1.0, 1.5, 2.0, 3.0, 4.0, 6.0, -0.0, -0.5, -1.0, -1.5, -2.0, -3.0, -4.0, -6.0])


def pack_weight(w, fmt):
    k, n = w.shape
    w = f64(np.asarray(w, np.float32).astype(ml_dtypes.bfloat16)).reshape(k // 32, 32, n)
    amax = np.abs(w).max(1)
    if fmt == "e4m3":
        byte = np.frexp(amax)[1] - 1 + 127 - 7
    else:
        mant, ex = np.frexp(amax / 6.0)
        byte = np.where(mant > 0.5, ex, ex - 1) + 127
    byte = np.clip(np.where(amax > 0, byte, 1), 1, 254)
    scaled = (w * np.exp2(127.0 - byte)[:, None, :]).reshape(k, n).astype(np.float32)
    by_word = np.ascontiguousarray(scaled.reshape(k // 512, 128, 4, n).transpose(0, 1, 3, 2))
    if fmt == "e4m3":
        words = by_word.astype(ml_dtypes.float8_e4m3fn).view(np.uint8)
    else:
        c = by_word.astype(ml_dtypes.float4_e2m1fn).view(np.uint8) & 0xF
        words = (c[..., 0::2] | (c[..., 1::2] << 4)).reshape(k // 512, 128, 2 * n)
    return np.ascontiguousarray(words), np.ascontiguousarray(byte.astype(np.uint8).reshape(k // 512, 16, n))


def unpack_weight(words, scales, fmt):
    g, _, n = scales.shape
    words = np.ascontiguousarray(words).reshape(g, 128, n, -1)
    if fmt == "e4m3":
        vals = words.view(ml_dtypes.float8_e4m3fn).astype(np.float64)
    else:
        nib = np.empty((g, 128, n, 4), np.uint8)
        nib[..., 0::2] = words & 0xF
        nib[..., 1::2] = words >> 4
        vals = E2M1[nib]
    vals = vals * np.repeat(np.exp2(scales.astype(np.float64) - 127.0), 8, axis=1)[..., None]
    return vals.transpose(0, 1, 3, 2).reshape(g * 512, n)


def sigmoid(v):
    return 1.0 / (1.0 + np.exp(-v))


D, E, T, I, Q, G = 512, 512, 2048, 512, 128, 32


def setup_inputs():
    n = np.random.standard_normal
    idx = np.random.permutation(T)[:I]
    fd = mx_kscale(D)
    fe = mx_kscale(E)
    keysp = pack_weight(n((D, T)) / fd[:, None], "e4m3")
    valsp = pack_weight(n((E, T)) / fe[:, None], "e4m3")
    return {
        "query": (n((D, Q)) * 0.7 / np.sqrt(D) * fd[:, None]).astype(np.float32),
        "keys_words": keysp[0],
        "keys_scales": keysp[1],
        "th": (np.random.uniform(-0.2, 0.2, (Q, 1))).astype(np.float32),
        "steep": (np.random.uniform(2.0, 8.0, (Q, 1))).astype(np.float32),
        "gout": (n((E, Q)) * 1 / np.sqrt(E) * fe[:, None]).astype(np.float32),
        "vals_words": valsp[0],
        "vals_scales": valsp[1],
        "size": (np.random.uniform(0.5, 2.0, (1, I))).astype(np.float32),
        "old": (0.5 * n((Q, T))).astype(np.float32),
        "offs": striped(idx),
    }


def reference(query, keys_words, keys_scales, th, steep, gout, vals_words, vals_scales, size, old, offs):
    idx = unstriped(offs)
    keysu = unpack_weight(keys_words, keys_scales, "e4m3")
    valsu = unpack_weight(vals_words, vals_scales, "e4m3")
    queryq = mxq(f64(query), 0, "e4m3")
    keysidxg = keysu[:, idx]
    a = queryq.T @ keysidxg
    s = a.reshape(Q, G, I // G).mean(axis=2)
    gt = sigmoid((s - f64(th)) * f64(steep))
    gr = np.repeat(gt, I // G, axis=1)
    r = np.exp(a - np.max(a, axis=1, keepdims=True))
    p = r * gr
    z = np.sum(p, axis=1, keepdims=True)
    goutq = mxq(f64(gout), 0, "e4m3")
    valsidxg = valsu[:, idx]
    c0 = goutq.T @ valsidxg
    dz = np.sum(c0 * p * f64(size) / np.square(z) * (-1.0), axis=1, keepdims=True)
    dp = c0 / z * f64(size) + dz
    dr = dp * gr
    dgr = dp * r
    dgt = dgr.reshape(Q, G, I // G).sum(axis=2)
    ds = dgt * gt * (1.0 - gt) * f64(steep)
    e1 = ds / 16.0
    r1 = np.repeat(e1, I // G, axis=1)
    da = dr * r + r1
    gs = da * 512.0
    gf = np.zeros((Q, T))
    gf[:, idx] = gs
    y = f64(old) + gf
    return y

@@ -1,0 +1,182 @@
+from contextlib import ExitStack
+
+import concourse.mybir as mybir
+from concourse.masks import make_identity
+
+F32 = mybir.dt.float32
+BF16 = mybir.dt.bfloat16
+I32 = mybir.dt.int32
+U32 = mybir.dt.uint32
+U16 = mybir.dt.uint16
+U8 = mybir.dt.uint8
+FP8X4 = mybir.dt.float8_e4m3fn_x4
+ALU = mybir.AluOpType
+ACT = mybir.ActivationFunctionType
+AX = mybir.AxisListType
+
+P = 128
+PACK = 4
+T = 2048
+I = 512
+Q = 128
+G = 32
+PAGE = 16
+HALF = I // 2
+BANK = 512
+OUT_CHUNKS = (256, 512, 512, 512, 256)
+
+FLOPS = 2 * 2 * 512 * Q * I
+
+
+def tile_attend_bpagegate_s_kernel(tc, query, keys_words, keys_scales, th, steep, gout, vals_words, vals_scales, size, old, offs, out):
+    nc = tc.nc
+    with ExitStack() as ctx:
+        sb = ctx.enter_context(tc.tile_pool(name="sb", bufs=1))
+        ps = ctx.enter_context(tc.psum_pool(name="ps", bufs=1))
+
+        def tile(name, shape, dtype, tag=None):
+            return sb.tile(shape, dtype, name=name, tag=tag or name, align_bytes=64)
+
+        offsets = sb.tile([P, I // 16], U16, name="offsets")
+        nc.sync.dma_start(offsets[:], offs)
+
+        k_bytes = tile("k_bytes", [P, T], U8)
+        v_bytes = tile("v_bytes", [P, T], U8)
+        window = tile("window", [P, T], F32)
+        zeros = tile("zeros", [P, P], F32, tag="slot_k")
+        ident = tile("ident", [P, P], F32)
+        nc.gpsimd.memset(zeros[:], 0.0)
+        nc.vector.memset(k_bytes[:].bitcast(I32), 0)
+        nc.vector.tensor_copy(ident[:], zeros[:])
+        make_identity(nc, ident[:], nomemset=True)
+        nc.vector.memset(window[:], 0.0)
+        nc.vector.memset(v_bytes[:].bitcast(I32), 0)
+
+        def load_scale_rows(dst, src):
+            for quad in range(4):
+                nc.sync.dma_start(dst[32 * quad : 32 * quad + 4, :].bitcast(I32), src[0, 4 * quad : 4 * quad + 4, :].bitcast(I32))
+
+        q_raw = tile("q_raw", [P, PACK, Q], F32, tag="slot_cols")
+        g_raw = tile("g_raw", [P, PACK, Q], F32, tag="slot_v")
+        nc.sync.dma_start(q_raw[:], query.rearrange("(p j) q -> p j q", j=PACK))
+        nc.sync.dma_start(g_raw[:], gout.rearrange("(p j) q -> p j q", j=PACK))
+        load_scale_rows(k_bytes, keys_scales)
+        k_words = tile("k_words", [P, T], U32, tag="slot_k")
+        nc.sync.dma_start(k_words[:].bitcast(I32), keys_words[0].rearrange("p n t -> p (n t)").bitcast(I32))
+        load_scale_rows(v_bytes, vals_scales)
+
+        grouped = tile("grouped", [P, 2 * Q, PACK], BF16, tag="slot_size")
+        codes = tile("codes", [P, 2 * Q], U32)
+        scales = tile("scales", [P, 2 * Q], U8)
+        nc.scalar.copy(grouped[:, :Q, :], q_raw[:].rearrange("p j q -> p q j"))
+        nc.scalar.copy(grouped[:, Q:, :], g_raw[:].rearrange("p j q -> p q j"))
+        q_codes, q_scales = codes[:, :Q], scales[:, :Q]
+        g_codes, g_scales = codes[:, Q:], scales[:, Q:]
+
+        cols_in = tile("cols_in", [P, 16], F32, tag="slot_cols")
+        th_col, steep_col = cols_in[:, 0:1], cols_in[:, 8:9]
+        nc.sync.dma_start(th_col, th)
+        nc.sync.dma_start(steep_col, steep)
+        v_words = tile("v_words", [P, T], U32, tag="slot_v")
+        nc.sync.dma_start(v_words[:].bitcast(I32), vals_words[0].rearrange("p n t -> p (n t)").bitcast(I32))
+
+        th_steep = tile("th_steep", [P, 1], F32)
+        steep16 = tile("steep16", [P, 1], F32)
+        neg_steep16 = tile("neg_steep16", [P, 1], F32)
+        size512 = tile("size512", [P, 4], F32)
+        nc.gpsimd.tensor_tensor(th_steep[:], th_col, steep_col, ALU.mult)
+        nc.gpsimd.tensor_scalar(steep16[:], steep_col, 1.0 / PAGE, 0.0, ALU.mult, ALU.add)
+        nc.gpsimd.tensor_scalar(neg_steep16[:], steep_col, -1.0 / PAGE, 0.0, ALU.mult, ALU.add)
+
+        def half_offsets(h):
+            return offsets[:, h * (HALF // 16) : (h + 1) * (HALF // 16)]
+
+        k_bytes_g = tile("k_bytes_g", [P, I], U8)
+        v_bytes_g = tile("v_bytes_g", [P, I], U8)
+        nc.vector.tensor_copy(k_bytes_g[:], k_bytes[:].indirect(offsets[:]))
+        nc.vector.quantize_mx(out=codes[:].bitcast(FP8X4), scales=scales[:], in_=grouped[:].rearrange("p q j -> p (q j)"))
+        size_cols = tile("size_cols", [P, 4], F32, tag="slot_size")
+        with nc.allow_non_contiguous_dma(reason="one float32 a slot, slots on the partitions"):
+            nc.sync.dma_start(size_cols[:], size[0].rearrange("(j p) -> p j", p=P))
+        nc.gpsimd.tensor_scalar(size512[:], size_cols[:], 512.0, 0.0, ALU.mult, ALU.add)
+
+        k_words_g = tile("k_words_g", [P, I], U32)
+        a_ps = ps.tile([P, BANK], F32, name="a_ps")
+        nc.vector.tensor_copy(k_words_g[:], k_words[:].indirect(offsets[:]))
+        old_sb = tile("old_sb", [P, T], F32, tag="slot_k")
+        nc.sync.dma_start(old_sb[:], old)
+        nc.tensor.matmul_mx(
+            out=a_ps[:], lhsT=q_codes.bitcast(FP8X4), lhsT_scale=q_scales,
+            rhs=k_words_g[:].bitcast(FP8X4), rhs_scale=k_bytes_g[:], start=True, stop=True,
+        )
+        nc.vector.tensor_copy(v_bytes_g[:], v_bytes[:].indirect(offsets[:]))
+        neg_a = tile("neg_a", [P, I], F32)
+        neg_max = tile("neg_max", [P, 1], F32)
+        a_page = tile("a_page", [P, G], F32)
+        nc.vector.tensor_reduce(a_page[:], a_ps[:].rearrange("p (g s) -> p g s", s=PAGE), AX.X, ALU.add)
+        nc.vector.tensor_scalar(neg_a[:], a_ps[:], -1.0, None, ALU.mult, ALU.min, accum_out=neg_max[:])
+        r = tile("r", [P, I], F32)
+        gate_exp = tile("gate_exp", [P, G], F32)
+        gate_den = tile("gate_den", [P, G], F32)
+        gate_slope = tile("gate_slope", [P, G], F32)
+        nc.scalar.activation(gate_exp[:], a_page[:], ACT.Exp, bias=th_steep[:], scale=neg_steep16[:])
+        nc.scalar.activation(gate_den[:], gate_exp[:], ACT.Identity, bias=1.0, scale=1.0)
+        nc.scalar.activation(r[:], neg_a[:], ACT.Exp, bias=neg_max[:], scale=-1.0)
+        gate = tile("gate", [P, G], F32)
+        nc.vector.reciprocal(gate[:], gate_den[:])
+        nc.scalar.activation(gate_slope[:], gate[:], ACT.Identity, bias=steep16[:], scale=neg_steep16[:])
+
+        v_words_g = [tile("v_words_g%d" % h, [P, HALF], U32) for h in range(2)]
+        c_ps = [ps.tile([P, BANK], F32, name="c_ps%d" % j) for j in range(4)]
+        u_t = [tile("u_t%d" % j, [P, Q], F32) for j in range(4)]
+        u_ps = ps.tile([P, BANK], F32, name="u_ps")
+        for h in range(2):
+            nc.vector.tensor_copy(v_words_g[h][:], v_words[:].indirect(half_offsets(h)))
+            for j in (2 * h, 2 * h + 1):
+                nc.tensor.matmul_mx(
+                    out=c_ps[j][:, :Q], lhsT=v_words_g[h][:, (j % 2) * P : (j % 2 + 1) * P].bitcast(FP8X4),
+                    lhsT_scale=v_bytes_g[:, j * P : (j + 1) * P],
+                    rhs=g_codes.bitcast(FP8X4), rhs_scale=g_scales, start=True, stop=True,
+                )
+                nc.scalar.activation(u_t[j][:], c_ps[j][:, :Q], ACT.Copy, scale=size512[:, j : j + 1])
+        for j in range(4):
+            nc.tensor.transpose(u_ps[:, j * P : (j + 1) * P], u_t[j][:], ident[:])
+
+
+        def by_page(t):
+            return t[:].rearrange("p (g s) -> p g s", s=PAGE)
+
+        def spread(t):
+            return t[:].unsqueeze(2).to_broadcast([P, G, PAGE])
+
+        p = tile("p", [P, I], F32, tag="slot_v")
+        z = tile("z", [P, 1], F32)
+        inv_z = tile("inv_z", [P, 1], F32)
+        nc.vector.scalar_tensor_tensor(by_page(p), by_page(r), 1.0, spread(gate), ALU.mult, ALU.mult, accum_out=z[:])
+        nc.vector.reciprocal(inv_z[:], z[:])
+        p_norm = tile("p_norm", [P, I], F32)
+        nc.scalar.activation(p_norm[:], p[:], ACT.Copy, scale=inv_z[:])
+
+        up = tile("up", [P, I], F32)
+        mean_u = tile("mean_u", [P, 1], F32)
+        nc.vector.scalar_tensor_tensor(up[:], u_ps[:], inv_z[:], p[:], ALU.mult, ALU.mult, accum_out=mean_u[:])
+        h_t = tile("h_t", [P, I], F32)
+        h_page = tile("h_page", [P, G], F32)
+        page_wide = tile("page_wide", [P, I], F32)
+        slots = [slice(h * HALF, (h + 1) * HALF) for h in range(2)]
+        pages = [slice(h * G // 2, (h + 1) * G // 2) for h in range(2)]
+        for h in range(2):
+            nc.vector.scalar_tensor_tensor(h_t[:, slots[h]], u_ps[:, slots[h]], mean_u[:], p_norm[:, slots[h]], ALU.subtract, ALU.mult)
+        for h in range(2):
+            nc.vector.tensor_reduce(h_page[:, pages[h]], by_page(h_t)[:, pages[h], :], AX.X, ALU.add)
+        for h in range(2):
+            nc.vector.tensor_tensor(by_page(page_wide)[:, pages[h], :], spread(h_page)[:, pages[h], :], spread(gate_slope)[:, pages[h], :], ALU.mult)
+        nc.vector.tensor_tensor(window[:].indirect(offsets[:]), h_t[:], page_wide[:], ALU.add)
+
+        c0 = 0
+        for n, width in enumerate(OUT_CHUNKS):
+            cols = slice(c0, c0 + width)
+            res = tile("res%d" % n, [P, width], F32)
+            nc.vector.tensor_tensor(res[:], window[:, cols], old_sb[:, cols], ALU.add)
+            nc.sync.dma_start(out[:, cols], res[:])
+            c0 = c0 + width

@@ -45,25 +45,25 @@ def tile_attend_bpagegate_s_kernel(tc, query, keys_words, keys_scales, th, steep
         window = tile("window", [P, T], F32)
         zeros = tile("zeros", [P, P], F32, tag="slot_k")
         ident = tile("ident", [P, P], F32)
-        nc.gpsimd.memset(zeros[:], 0.0)
+        nc.vector.memset(zeros[:], 0.0)
         nc.vector.memset(k_bytes[:].bitcast(I32), 0)
         nc.vector.tensor_copy(ident[:], zeros[:])
         make_identity(nc, ident[:], nomemset=True)
-        nc.vector.memset(window[:], 0.0)
         nc.vector.memset(v_bytes[:].bitcast(I32), 0)
+        nc.vector.memset(window[:], 0.0)
 
-        def load_scale_rows(dst, src):
+        def load_scale_rows(dst, src, queues):
             for quad in range(4):
-                nc.sync.dma_start(dst[32 * quad : 32 * quad + 4, :].bitcast(I32), src[0, 4 * quad : 4 * quad + 4, :].bitcast(I32))
+                queues[quad % len(queues)].dma_start(dst[32 * quad : 32 * quad + 4, :].bitcast(I32), src[0, 4 * quad : 4 * quad + 4, :].bitcast(I32))
 
         q_raw = tile("q_raw", [P, PACK, Q], F32, tag="slot_cols")
         g_raw = tile("g_raw", [P, PACK, Q], F32, tag="slot_v")
-        nc.sync.dma_start(q_raw[:], query.rearrange("(p j) q -> p j q", j=PACK))
-        nc.sync.dma_start(g_raw[:], gout.rearrange("(p j) q -> p j q", j=PACK))
-        load_scale_rows(k_bytes, keys_scales)
+        nc.scalar.dma_start(q_raw[:], query.rearrange("(p j) q -> p j q", j=PACK))
+        nc.scalar.dma_start(g_raw[:], gout.rearrange("(p j) q -> p j q", j=PACK))
+        load_scale_rows(k_bytes, keys_scales, (nc.sync, nc.scalar))
         k_words = tile("k_words", [P, T], U32, tag="slot_k")
         nc.sync.dma_start(k_words[:].bitcast(I32), keys_words[0].rearrange("p n t -> p (n t)").bitcast(I32))
-        load_scale_rows(v_bytes, vals_scales)
+        load_scale_rows(v_bytes, vals_scales, (nc.sync,))
 
         grouped = tile("grouped", [P, 2 * Q, PACK], BF16, tag="slot_size")
         codes = tile("codes", [P, 2 * Q], U32)
@@ -100,31 +100,42 @@ def tile_attend_bpagegate_s_kernel(tc, query, keys_words, keys_scales, th, steep
             nc.sync.dma_start(size_cols[:], size[0].rearrange("(j p) -> p j", p=P))
         nc.gpsimd.tensor_scalar(size512[:], size_cols[:], 512.0, 0.0, ALU.mult, ALU.add)
 
-        k_words_g = tile("k_words_g", [P, I], U32)
-        a_ps = ps.tile([P, BANK], F32, name="a_ps")
-        nc.vector.tensor_copy(k_words_g[:], k_words[:].indirect(offsets[:]))
+        slots = [slice(h * HALF, (h + 1) * HALF) for h in range(2)]
+        pages = [slice(h * G // 2, (h + 1) * G // 2) for h in range(2)]
+        k_words_g = [tile("k_words_g%d" % h, [P, HALF], U32) for h in range(2)]
+        a_ps = [ps.tile([P, BANK], F32, name="a_ps%d" % h) for h in range(2)]
+        for h in range(2):
+            nc.vector.tensor_copy(k_words_g[h][:], k_words[:].indirect(half_offsets(h)))
+            nc.tensor.matmul_mx(
+                out=a_ps[h][:, :HALF], lhsT=q_codes.bitcast(FP8X4), lhsT_scale=q_scales,
+                rhs=k_words_g[h][:].bitcast(FP8X4), rhs_scale=k_bytes_g[:, slots[h]], start=True, stop=True,
+            )
         old_sb = tile("old_sb", [P, T], F32, tag="slot_k")
         nc.sync.dma_start(old_sb[:], old)
-        nc.tensor.matmul_mx(
-            out=a_ps[:], lhsT=q_codes.bitcast(FP8X4), lhsT_scale=q_scales,
-            rhs=k_words_g[:].bitcast(FP8X4), rhs_scale=k_bytes_g[:], start=True, stop=True,
-        )
-        nc.vector.tensor_copy(v_bytes_g[:], v_bytes[:].indirect(offsets[:]))
         neg_a = tile("neg_a", [P, I], F32)
-        neg_max = tile("neg_max", [P, 1], F32)
         a_page = tile("a_page", [P, G], F32)
-        nc.vector.tensor_reduce(a_page[:], a_ps[:].rearrange("p (g s) -> p g s", s=PAGE), AX.X, ALU.add)
-        nc.vector.tensor_scalar(neg_a[:], a_ps[:], -1.0, None, ALU.mult, ALU.min, accum_out=neg_max[:])
+        neg_max = [tile("neg_max%d" % h, [P, 1], F32) for h in range(2)]
+        for h in range(2):
+            so_far = neg_max[0][:] if h else None
+            nc.vector.tensor_scalar(neg_a[:, slots[h]], a_ps[h][:, :HALF], -1.0, so_far, ALU.mult, ALU.min, accum_out=neg_max[h][:])
+            nc.vector.tensor_reduce(a_page[:, pages[h]], a_ps[h][:, :HALF].rearrange("p (g s) -> p g s", s=PAGE), AX.X, ALU.add)
+        nc.vector.tensor_copy(v_bytes_g[:], v_bytes[:].indirect(offsets[:]))
         r = tile("r", [P, I], F32)
-        gate_exp = tile("gate_exp", [P, G], F32)
-        gate_den = tile("gate_den", [P, G], F32)
-        gate_slope = tile("gate_slope", [P, G], F32)
-        nc.scalar.activation(gate_exp[:], a_page[:], ACT.Exp, bias=th_steep[:], scale=neg_steep16[:])
-        nc.scalar.activation(gate_den[:], gate_exp[:], ACT.Identity, bias=1.0, scale=1.0)
-        nc.scalar.activation(r[:], neg_a[:], ACT.Exp, bias=neg_max[:], scale=-1.0)
+        below = tile("below", [P, G], F32)
+        distance = tile("distance", [P, G], F32)
+        low_factor = tile("low_factor", [P, G], F32)
+        tanh_half = tile("tanh_half", [P, G], F32)
+        high_factor = tile("high_factor", [P, G], F32)
         gate = tile("gate", [P, G], F32)
-        nc.vector.reciprocal(gate[:], gate_den[:])
-        nc.scalar.activation(gate_slope[:], gate[:], ACT.Identity, bias=steep16[:], scale=neg_steep16[:])
+        gate_slope = tile("gate_slope", [P, G], F32)
+        nc.scalar.activation(r[:], neg_a[:], ACT.Exp, bias=neg_max[1][:], scale=-1.0)
+        nc.scalar.activation(below[:], a_page[:], ACT.Relu, bias=th_steep[:], scale=neg_steep16[:])
+        nc.scalar.activation(distance[:], a_page[:], ACT.Abs, bias=th_steep[:], scale=neg_steep16[:])
+        nc.scalar.activation(low_factor[:], below[:], ACT.Exp, scale=-1.0)
+        nc.scalar.activation(tanh_half[:], distance[:], ACT.Tanh, scale=0.5)
+        nc.gpsimd.tensor_scalar(high_factor[:], tanh_half[:], 0.5, 0.5, ALU.mult, ALU.add)
+        nc.gpsimd.tensor_tensor(gate[:], low_factor[:], high_factor[:], ALU.mult)
+        nc.gpsimd.tensor_scalar(gate_slope[:], gate[:], neg_steep16[:], steep16[:], ALU.mult, ALU.add)
 
         v_words_g = [tile("v_words_g%d" % h, [P, HALF], U32) for h in range(2)]
         c_ps = [ps.tile([P, BANK], F32, name="c_ps%d" % j) for j in range(4)]
@@ -149,7 +160,7 @@ def tile_attend_bpagegate_s_kernel(tc, query, keys_words, keys_scales, th, steep
         def spread(t):
             return t[:].unsqueeze(2).to_broadcast([P, G, PAGE])
 
-        p = tile("p", [P, I], F32, tag="slot_v")
+        p = tile("p", [P, I], F32, tag="v_words_g0")
         z = tile("z", [P, 1], F32)
         inv_z = tile("inv_z", [P, 1], F32)
         nc.vector.scalar_tensor_tensor(by_page(p), by_page(r), 1.0, spread(gate), ALU.mult, ALU.mult, accum_out=z[:])
@@ -163,8 +174,6 @@ def tile_attend_bpagegate_s_kernel(tc, query, keys_words, keys_scales, th, steep
         h_t = tile("h_t", [P, I], F32)
         h_page = tile("h_page", [P, G], F32)
         page_wide = tile("page_wide", [P, I], F32)
-        slots = [slice(h * HALF, (h + 1) * HALF) for h in range(2)]
-        pages = [slice(h * G // 2, (h + 1) * G // 2) for h in range(2)]
         for h in range(2):
             nc.vector.scalar_tensor_tensor(h_t[:, slots[h]], u_ps[:, slots[h]], mean_u[:], p_norm[:, slots[h]], ALU.subtract, ALU.mult)
         for h in range(2):

from contextlib import ExitStack

import concourse.mybir as mybir
from concourse.masks import make_identity

F32 = mybir.dt.float32
BF16 = mybir.dt.bfloat16
I32 = mybir.dt.int32
U32 = mybir.dt.uint32
U16 = mybir.dt.uint16
U8 = mybir.dt.uint8
FP8X4 = mybir.dt.float8_e4m3fn_x4
ALU = mybir.AluOpType
ACT = mybir.ActivationFunctionType
AX = mybir.AxisListType

P = 128
PACK = 4
T = 2048
I = 512
Q = 128
G = 32
PAGE = 16
HALF = I // 2
BANK = 512
OUT_CHUNKS = (256, 512, 512, 512, 256)

FLOPS = 2 * 2 * 512 * Q * I


def tile_attend_bpagegate_s_kernel(tc, query, keys_words, keys_scales, th, steep, gout, vals_words, vals_scales, size, old, offs, out):
    nc = tc.nc
    with ExitStack() as ctx:
        sb = ctx.enter_context(tc.tile_pool(name="sb", bufs=1))
        ps = ctx.enter_context(tc.psum_pool(name="ps", bufs=1))

        def tile(name, shape, dtype, tag=None):
            return sb.tile(shape, dtype, name=name, tag=tag or name, align_bytes=64)

        offsets = sb.tile([P, I // 16], U16, name="offsets")
        nc.sync.dma_start(offsets[:], offs)

        k_bytes = tile("k_bytes", [P, T], U8)
        v_bytes = tile("v_bytes", [P, T], U8)
        window = tile("window", [P, T], F32)
        zeros = tile("zeros", [P, P], F32, tag="slot_k")
        ident = tile("ident", [P, P], F32)
        nc.vector.memset(zeros[:], 0.0)
        nc.vector.memset(k_bytes[:].bitcast(I32), 0)
        nc.vector.tensor_copy(ident[:], zeros[:])
        make_identity(nc, ident[:], nomemset=True)
        nc.vector.memset(v_bytes[:].bitcast(I32), 0)
        nc.vector.memset(window[:], 0.0)

        def load_scale_rows(dst, src, queues):
            for quad in range(4):
                queues[quad % len(queues)].dma_start(dst[32 * quad : 32 * quad + 4, :].bitcast(I32), src[0, 4 * quad : 4 * quad + 4, :].bitcast(I32))

        q_raw = tile("q_raw", [P, PACK, Q], F32, tag="slot_cols")
        g_raw = tile("g_raw", [P, PACK, Q], F32, tag="slot_v")
        nc.scalar.dma_start(q_raw[:], query.rearrange("(p j) q -> p j q", j=PACK))
        nc.scalar.dma_start(g_raw[:], gout.rearrange("(p j) q -> p j q", j=PACK))
        load_scale_rows(k_bytes, keys_scales, (nc.sync, nc.scalar))
        k_words = tile("k_words", [P, T], U32, tag="slot_k")
        nc.sync.dma_start(k_words[:].bitcast(I32), keys_words[0].rearrange("p n t -> p (n t)").bitcast(I32))
        load_scale_rows(v_bytes, vals_scales, (nc.sync,))

        grouped = tile("grouped", [P, 2 * Q, PACK], BF16, tag="slot_size")
        codes = tile("codes", [P, 2 * Q], U32)
        scales = tile("scales", [P, 2 * Q], U8)
        nc.scalar.copy(grouped[:, :Q, :], q_raw[:].rearrange("p j q -> p q j"))
        nc.scalar.copy(grouped[:, Q:, :], g_raw[:].rearrange("p j q -> p q j"))
        q_codes, q_scales = codes[:, :Q], scales[:, :Q]
        g_codes, g_scales = codes[:, Q:], scales[:, Q:]

        cols_in = tile("cols_in", [P, 16], F32, tag="slot_cols")
        th_col, steep_col = cols_in[:, 0:1], cols_in[:, 8:9]
        nc.sync.dma_start(th_col, th)
        nc.sync.dma_start(steep_col, steep)
        v_words = tile("v_words", [P, T], U32, tag="slot_v")
        nc.sync.dma_start(v_words[:].bitcast(I32), vals_words[0].rearrange("p n t -> p (n t)").bitcast(I32))

        th_steep = tile("th_steep", [P, 1], F32)
        steep16 = tile("steep16", [P, 1], F32)
        neg_steep16 = tile("neg_steep16", [P, 1], F32)
        size512 = tile("size512", [P, 4], F32)
        nc.gpsimd.tensor_tensor(th_steep[:], th_col, steep_col, ALU.mult)
        nc.gpsimd.tensor_scalar(steep16[:], steep_col, 1.0 / PAGE, 0.0, ALU.mult, ALU.add)
        nc.gpsimd.tensor_scalar(neg_steep16[:], steep_col, -1.0 / PAGE, 0.0, ALU.mult, ALU.add)

        def half_offsets(h):
            return offsets[:, h * (HALF // 16) : (h + 1) * (HALF // 16)]

        k_bytes_g = tile("k_bytes_g", [P, I], U8)
        v_bytes_g = tile("v_bytes_g", [P, I], U8)
        nc.vector.tensor_copy(k_bytes_g[:], k_bytes[:].indirect(offsets[:]))
        nc.vector.quantize_mx(out=codes[:].bitcast(FP8X4), scales=scales[:], in_=grouped[:].rearrange("p q j -> p (q j)"))
        size_cols = tile("size_cols", [P, 4], F32, tag="slot_size")
        with nc.allow_non_contiguous_dma(reason="one float32 a slot, slots on the partitions"):
            nc.sync.dma_start(size_cols[:], size[0].rearrange("(j p) -> p j", p=P))
        nc.gpsimd.tensor_scalar(size512[:], size_cols[:], 512.0, 0.0, ALU.mult, ALU.add)

        slots = [slice(h * HALF, (h + 1) * HALF) for h in range(2)]
        pages = [slice(h * G // 2, (h + 1) * G // 2) for h in range(2)]
        k_words_g = [tile("k_words_g%d" % h, [P, HALF], U32) for h in range(2)]
        a_ps = [ps.tile([P, BANK], F32, name="a_ps%d" % h) for h in range(2)]
        for h in range(2):
            nc.vector.tensor_copy(k_words_g[h][:], k_words[:].indirect(half_offsets(h)))
            nc.tensor.matmul_mx(
                out=a_ps[h][:, :HALF], lhsT=q_codes.bitcast(FP8X4), lhsT_scale=q_scales,
                rhs=k_words_g[h][:].bitcast(FP8X4), rhs_scale=k_bytes_g[:, slots[h]], start=True, stop=True,
            )
        old_sb = tile("old_sb", [P, T], F32, tag="slot_k")
        nc.sync.dma_start(old_sb[:], old)
        neg_a = tile("neg_a", [P, I], F32)
        a_page = tile("a_page", [P, G], F32)
        neg_max = [tile("neg_max%d" % h, [P, 1], F32) for h in range(2)]
        for h in range(2):
            so_far = neg_max[0][:] if h else None
            nc.vector.tensor_scalar(neg_a[:, slots[h]], a_ps[h][:, :HALF], -1.0, so_far, ALU.mult, ALU.min, accum_out=neg_max[h][:])
            nc.vector.tensor_reduce(a_page[:, pages[h]], a_ps[h][:, :HALF].rearrange("p (g s) -> p g s", s=PAGE), AX.X, ALU.add)
        nc.vector.tensor_copy(v_bytes_g[:], v_bytes[:].indirect(offsets[:]))
        r = tile("r", [P, I], F32)
        below = tile("below", [P, G], F32)
        distance = tile("distance", [P, G], F32)
        low_factor = tile("low_factor", [P, G], F32)
        tanh_half = tile("tanh_half", [P, G], F32)
        high_factor = tile("high_factor", [P, G], F32)
        gate = tile("gate", [P, G], F32)
        gate_slope = tile("gate_slope", [P, G], F32)
        nc.scalar.activation(r[:], neg_a[:], ACT.Exp, bias=neg_max[1][:], scale=-1.0)
        nc.scalar.activation(below[:], a_page[:], ACT.Relu, bias=th_steep[:], scale=neg_steep16[:])
        nc.scalar.activation(distance[:], a_page[:], ACT.Abs, bias=th_steep[:], scale=neg_steep16[:])
        nc.scalar.activation(low_factor[:], below[:], ACT.Exp, scale=-1.0)
        nc.scalar.activation(tanh_half[:], distance[:], ACT.Tanh, scale=0.5)
        nc.gpsimd.tensor_scalar(high_factor[:], tanh_half[:], 0.5, 0.5, ALU.mult, ALU.add)
        nc.gpsimd.tensor_tensor(gate[:], low_factor[:], high_factor[:], ALU.mult)
        nc.gpsimd.tensor_scalar(gate_slope[:], gate[:], neg_steep16[:], steep16[:], ALU.mult, ALU.add)

        v_words_g = [tile("v_words_g%d" % h, [P, HALF], U32) for h in range(2)]
        c_ps = [ps.tile([P, BANK], F32, name="c_ps%d" % j) for j in range(4)]
        u_t = [tile("u_t%d" % j, [P, Q], F32) for j in range(4)]
        u_ps = ps.tile([P, BANK], F32, name="u_ps")
        for h in range(2):
            nc.vector.tensor_copy(v_words_g[h][:], v_words[:].indirect(half_offsets(h)))
            for j in (2 * h, 2 * h + 1):
                nc.tensor.matmul_mx(
                    out=c_ps[j][:, :Q], lhsT=v_words_g[h][:, (j % 2) * P : (j % 2 + 1) * P].bitcast(FP8X4),
                    lhsT_scale=v_bytes_g[:, j * P : (j + 1) * P],
                    rhs=g_codes.bitcast(FP8X4), rhs_scale=g_scales, start=True, stop=True,
                )
                nc.scalar.activation(u_t[j][:], c_ps[j][:, :Q], ACT.Copy, scale=size512[:, j : j + 1])
        for j in range(4):
            nc.tensor.transpose(u_ps[:, j * P : (j + 1) * P], u_t[j][:], ident[:])


        def by_page(t):
            return t[:].rearrange("p (g s) -> p g s", s=PAGE)

        def spread(t):
            return t[:].unsqueeze(2).to_broadcast([P, G, PAGE])

        p = tile("p", [P, I], F32, tag="v_words_g0")
        z = tile("z", [P, 1], F32)
        inv_z = tile("inv_z", [P, 1], F32)
        nc.vector.scalar_tensor_tensor(by_page(p), by_page(r), 1.0, spread(gate), ALU.mult, ALU.mult, accum_out=z[:])
        nc.vector.reciprocal(inv_z[:], z[:])
        p_norm = tile("p_norm", [P, I], F32)
        nc.scalar.activation(p_norm[:], p[:], ACT.Copy, scale=inv_z[:])

        up = tile("up", [P, I], F32)
        mean_u = tile("mean_u", [P, 1], F32)
        nc.vector.scalar_tensor_tensor(up[:], u_ps[:], inv_z[:], p[:], ALU.mult, ALU.mult, accum_out=mean_u[:])
        h_t = tile("h_t", [P, I], F32)
        h_page = tile("h_page", [P, G], F32)
        page_wide = tile("page_wide", [P, I], F32)
        for h in range(2):
            nc.vector.scalar_tensor_tensor(h_t[:, slots[h]], u_ps[:, slots[h]], mean_u[:], p_norm[:, slots[h]], ALU.subtract, ALU.mult)
        for h in range(2):
            nc.vector.tensor_reduce(h_page[:, pages[h]], by_page(h_t)[:, pages[h], :], AX.X, ALU.add)
        for h in range(2):
            nc.vector.tensor_tensor(by_page(page_wide)[:, pages[h], :], spread(h_page)[:, pages[h], :], spread(gate_slope)[:, pages[h], :], ALU.mult)
        nc.vector.tensor_tensor(window[:].indirect(offsets[:]), h_t[:], page_wide[:], ALU.add)

        c0 = 0
        for n, width in enumerate(OUT_CHUNKS):
            cols = slice(c0, c0 + width)
            res = tile("res%d" % n, [P, width], F32)
            nc.vector.tensor_tensor(res[:], window[:, cols], old_sb[:, cols], ALU.add)
            nc.sync.dma_start(out[:, cols], res[:])
            c0 = c0 + width
